import numpy as np
import ml_dtypes


def mxq(x, axis, fmt="e4m3"):
    dtype, down = {"e4m3": (ml_dtypes.float8_e4m3fn, 7), "e5m2": (ml_dtypes.float8_e5m2, 14)}[fmt]
    v = np.moveaxis(np.asarray(x, np.float32).astype(ml_dtypes.bfloat16).astype(np.float64), axis, -1)
    blocks = v.reshape(v.shape[:-1] + (-1, 32))
    amax = np.abs(blocks).max(-1, keepdims=True)
    byte = np.maximum(np.where(amax > 0, np.frexp(amax)[1] - 1 + 127, 0) - down, 1)
    scale = np.exp2(byte - 127.0)
    codes = (blocks / scale).astype(np.float32).astype(dtype).astype(np.float64)
    return np.moveaxis((codes * scale).reshape(v.shape), -1, axis)


WIDE = False


def mx_kscale(k):
    if not WIDE:
        return np.ones(k)
    levels = np.array([10, -10, 5, -5, 0])
    if k % 512:
        return np.exp2(np.random.permutation(np.resize(levels, k // 32))).repeat(32)
    a = np.empty((k // 512, 16))
    for p in range(k // 512):
        a[p, :8] = np.random.permutation(np.resize(levels, 8))
        for g in range(8):
            far = levels[np.abs(levels - a[p, g]) >= 10]
            a[p, g + 8] = far[np.random.randint(len(far))]
    return np.exp2(a.ravel()).repeat(32)


def f64(x):
    return np.asarray(x).astype(np.float64)


def striped(idx):
    return np.tile(idx.reshape(-1, 16).T, (8, 1)).astype(np.uint16)


def unstriped(offs):
    return offs[:16].T.reshape(-1).astype(np.int64)


def striped8(idx):
    return np.concatenate([x.reshape(-1, 16).T for x in idx]).astype(np.uint16)


def runs(offs, k):
    lists = np.stack([offs[16 * r : 16 * r + 16].T.reshape(-1) for r in range(8)]).astype(np.int64)
    return lists[np.arange(k) % 512 // 64]


def pack_weight(w):
    k, n = w.shape
    w = f64(np.asarray(w, np.float32).astype(ml_dtypes.bfloat16)).reshape(k // 32, 32, n)
    amax = np.abs(w).max(1)
    byte = np.clip(np.where(amax > 0, np.frexp(amax)[1] - 1 + 127 - 7, 1), 1, 254)
    scaled = (w * np.exp2(127.0 - byte)[:, None, :]).reshape(k, n).astype(np.float32)
    words = np.ascontiguousarray(scaled.reshape(k // 512, 128, 4, n).transpose(0, 1, 3, 2)).astype(ml_dtypes.float8_e4m3fn).view(np.uint8)
    return words, np.ascontiguousarray(byte.astype(np.uint8).reshape(k // 512, 16, n))


def unpack_weight(words, scales):
    g, p, n, _ = words.shape
    vals = np.ascontiguousarray(words).view(ml_dtypes.float8_e4m3fn).astype(np.float64) * np.repeat(np.exp2(scales.astype(np.float64) - 127.0), 8, axis=1)[..., None]
    return vals.transpose(0, 1, 3, 2).reshape(g * 512, n)


E2M1 = np.array([0.0, 0.5, 1.0, 1.5, 2.0, 3.0, 4.0, 6.0, -0.0, -0.5, -1.0, -1.5, -2.0, -3.0, -4.0, -6.0])


def pack_fp4(w):
    k, n = w.shape
    w = f64(np.asarray(w, np.float32).astype(ml_dtypes.bfloat16)).reshape(k // 32, 32, n)
    amax = np.abs(w).max(1)
    mant, ex = np.frexp(amax / 6.0)
    byte = np.clip(np.where(amax > 0, np.where(mant > 0.5, ex, ex - 1) + 127, 1), 1, 254)
    scaled = (w * np.exp2(127.0 - byte)[:, None, :]).reshape(k, n).astype(np.float32)
    c = np.ascontiguousarray(scaled.reshape(k // 512, 128, 4, n).transpose(0, 1, 3, 2)).astype(ml_dtypes.float4_e2m1fn).view(np.uint8) & 0xF
    words = (c[..., 0::2] | (c[..., 1::2] << 4)).reshape(k // 512, 128, 2 * n)
    return np.ascontiguousarray(words), np.ascontiguousarray(byte.astype(np.uint8).reshape(k // 512, 16, n))


def unpack_fp4(words, scales):
    g, _, n = scales.shape
    words = np.ascontiguousarray(words).reshape(g, 128, n, 2)
    nib = np.empty((g, 128, n, 4), np.uint8)
    nib[..., 0::2] = words & 0xF
    nib[..., 1::2] = words >> 4
    vals = E2M1[nib] * np.repeat(np.exp2(scales.astype(np.float64) - 127.0), 8, axis=1)[..., None]
    return vals.transpose(0, 1, 3, 2).reshape(g * 512, n)


def sigmoid(v):
    return 1.0 / (1.0 + np.exp(-np.maximum(v, -700.0)))

def planes(y):
    n, m = y.shape
    v = y.astype(np.float32).astype(ml_dtypes.bfloat16).astype(np.float64).reshape(n // 32, 32, m)
    top = np.abs(v).max(1)
    byte = np.clip(np.where(top > 0, np.frexp(top)[1] - 1 + 127 - 7, 1), 1, 254)
    codes = (v * np.exp2(127.0 - byte)[:, None, :]).reshape(n, m).astype(np.float32).astype(ml_dtypes.float8_e4m3fn).view(np.uint8)
    words = codes.reshape(n // 512, 128, 4, m).transpose(0, 1, 3, 2)
    return np.ascontiguousarray(words), np.ascontiguousarray(byte.astype(np.uint8).reshape(n // 512, 16, m))


K, T, S, N, H = 512, 2048, 512, 512, 512


def setup_inputs():
    n = np.random.standard_normal
    s = mx_kscale(K)[:, None]
    u = mx_kscale(H)
    packed_xT = pack_weight(n((K, T)) * s)
    packed_w1 = pack_fp4(n((K, H)) / np.sqrt(K) / s)
    packed_w2 = pack_fp4(n((H, N)) / np.sqrt(H) / u[:, None])
    packed_w3 = pack_fp4(n((H, N)) / np.sqrt(H) / u[:, None])
    return {
        "x_words": packed_xT[0],
        "x_scales": packed_xT[1],
        "w1_words": packed_w1[0],
        "w1_scales": packed_w1[1],
        "gn": (np.random.uniform(0.5, 1.5, (H, 1)) * u[:, None]).astype(np.float32),
        "w2_words": packed_w2[0],
        "w2_scales": packed_w2[1],
        "gm": (np.random.uniform(0.5, 1.5, (H, 1)) * u[:, None]).astype(np.float32),
        "w3_words": packed_w3[0],
        "w3_scales": packed_w3[1],
        "offs": striped(np.random.permutation(T)[:S]),
        "n1": striped8(np.stack([np.random.permutation(S) for _ in range(8)])),
        "n2": striped8(np.stack([np.random.permutation(S) for _ in range(8)])),
        "n3": striped8(np.stack([np.random.permutation(S) for _ in range(8)])),
        "n4": striped8(np.stack([np.random.permutation(S) for _ in range(8)])),
        "n5": striped8(np.stack([np.random.permutation(S) for _ in range(8)])),
        "n6": striped8(np.stack([np.random.permutation(S) for _ in range(8)])),
    }


def reference(x_words, x_scales, w1_words, w1_scales, gn, w2_words, w2_scales, gm, w3_words, w3_scales, offs, n1, n2, n3, n4, n5, n6):
    xq = unpack_weight(x_words, x_scales)[:, unstriped(offs)]
    y = unpack_fp4(w1_words, w1_scales).T @ xq
    z = f64(gn) * (y * (sigmoid(y[np.arange(H)[:, None], runs(n1, H)] - (y[np.arange(H)[:, None], runs(n2, H)]))))
    a = unpack_fp4(w2_words, w2_scales).T @ mxq(z, 0, "e4m3")
    st = np.maximum(y, y[np.arange(H)[:, None], runs(n3, H)])
    z2 = f64(gm) * (np.minimum(st, st[np.arange(H)[:, None], runs(n4, H)]))
    b = unpack_fp4(w3_words, w3_scales).T @ mxq(z2, 0, "e4m3")
    out_0 = (a + a[np.arange(N)[:, None], runs(n5, N)]) * (sigmoid(b + b[np.arange(N)[:, None], runs(n6, N)]))
    return (out_0,) + planes(out_0)

@@ -1,0 +1,261 @@
+from contextlib import ExitStack
+
+import concourse.mybir as mybir
+
+K, T, S, N, H = 512, 2048, 512, 512, 512
+FLOPS = 3 * 2 * 512 * 512 * 512
+
+F32 = mybir.dt.float32
+BF16 = mybir.dt.bfloat16
+I32 = mybir.dt.int32
+U32 = mybir.dt.uint32
+U16 = mybir.dt.uint16
+U8 = mybir.dt.uint8
+FP8X4 = mybir.dt.float8_e4m3fn_x4
+FP4X4 = mybir.dt.float4_e2m1fn_x4
+ALU = mybir.AluOpType
+ACT = mybir.ActivationFunctionType
+
+P = 128
+PACK = 4
+OUT_CHUNKS = ((0, 256), (256, 128), (384, 128))
+
+
+def load_scale_rows(queue, plane, rows):
+    for q in range(4):
+        queue.dma_start(out=plane[32 * q : 32 * q + 4, :].bitcast(I32), in_=rows[0, 4 * q : 4 * q + 4, :].bitcast(I32))
+
+
+def tile_picked_forktriebcmphopmn_none_po_kernel(
+    tc, x_words, x_scales, w1_words, w1_scales, gn, w2_words, w2_scales, gm, w3_words, w3_scales,
+    offs, n1, n2, n3, n4, n5, n6, out_0, out_1, out_2,
+):
+    nc = tc.nc
+    with ExitStack() as ctx:
+        held = ctx.enter_context(tc.tile_pool(name="held", bufs=1))
+        ring = ctx.enter_context(tc.tile_pool(name="ring", bufs=2))
+        psum = ctx.enter_context(tc.psum_pool(name="psum", bufs=8))
+
+        def list_tile(name):
+            return held.tile([P, S // 16], U16, name=name)
+
+        offs_sb = list_tile("offs_sb")
+        n_sb = [list_tile("n%d_sb" % i) for i in range(1, 7)]
+        n1_sb, n2_sb, n3_sb, n4_sb, n5_sb, n6_sb = n_sb
+
+        xw = held.tile([P, T], I32, name="xw", align_bytes=64)
+        xs = held.tile([P, T], U8, name="xs", align_bytes=64)
+        raw_w = [held.tile([P, 2 * H], U8, name="raw_w%d" % i, align_bytes=64) for i in range(3)]
+        raw_s = [held.tile([P, H], U8, name="raw_s%d" % i, align_bytes=64) for i in range(3)]
+        deal_w = [held.tile([P, 2 * H], U8, name="deal_w%d" % i, align_bytes=64) for i in range(3)]
+        deal_s = [held.tile([P, H], U8, name="deal_s%d" % i, align_bytes=64) for i in range(3)]
+        gn_sb = held.tile([P, PACK], F32, name="gn_sb")
+        gm_sb = held.tile([P, PACK], F32, name="gm_sb")
+        y_win = [held.tile([P, 2 * S], F32, name="y_win%d" % t) for t in range(PACK)]
+        st_win = [held.tile([P, 2 * S], F32, name="st_win%d" % t) for t in range(PACK)]
+
+        nc.vector.memset(xs[:].bitcast(I32), 0)
+        nc.vector.memset(raw_s[0][:].bitcast(I32), 0)
+        nc.vector.memset(raw_s[2][:].bitcast(I32), 0)
+        nc.vector.memset(raw_s[1][:].bitcast(I32), 0)
+        for t in range(PACK):
+            nc.vector.memset(y_win[t][:, S:], 0.0)
+            nc.gpsimd.memset(st_win[t][:, S:], 0.0)
+
+        w_words = (w1_words, w2_words, w3_words)
+        w_scales = (w1_scales, w2_scales, w3_scales)
+
+        def load_words(i):
+            nc.sync.dma_start(out=raw_w[i][:].bitcast(I32), in_=w_words[i][0].bitcast(I32))
+
+        nc.sync.dma_start(offs_sb[:], offs)
+        nc.sync.dma_start(out=xw[:], in_=x_words[0].rearrange("p c r -> p (c r)").bitcast(I32))
+        load_words(0)
+        load_scale_rows(nc.sync, xs, x_scales)
+        load_scale_rows(nc.sync, raw_s[0], w_scales[0])
+        load_words(2)
+        load_words(1)
+        nc.sync.dma_start(n3_sb[:], n3)
+        nc.sync.dma_start(n4_sb[:], n4)
+        nc.sync.dma_start(out=gm_sb[:], in_=gm.rearrange("(p t) o -> p (t o)", t=PACK))
+        nc.sync.dma_start(out=gn_sb[:], in_=gn.rearrange("(p t) o -> p (t o)", t=PACK))
+        load_scale_rows(nc.sync, raw_s[2], w_scales[2])
+        load_scale_rows(nc.sync, raw_s[1], w_scales[1])
+        nc.sync.dma_start(n1_sb[:], n1)
+        nc.sync.dma_start(n2_sb[:], n2)
+        nc.sync.dma_start(n6_sb[:], n6)
+        nc.sync.dma_start(n5_sb[:], n5)
+
+        def deal_words(i):
+            nc.vector.tensor_copy(
+                out=deal_w[i][:].rearrange("p (t m b) -> p t m b", t=PACK, b=2),
+                in_=raw_w[i][:].rearrange("p (m t b) -> p t m b", t=PACK, b=2),
+            )
+
+        def deal_scales(i):
+            nc.vector.tensor_copy(
+                out=deal_s[i][:].rearrange("p (t m) -> p t m", t=PACK),
+                in_=raw_s[i][:].rearrange("p (m t) -> p t m", t=PACK),
+            )
+
+        def product(i, t, acc, codes, scales):
+            nc.tensor.matmul_mx(
+                out=acc,
+                lhsT=deal_w[i][:, 2 * P * t : 2 * P * (t + 1)].bitcast(FP4X4),
+                lhsT_scale=deal_s[i][:, P * t : P * (t + 1)],
+                rhs=codes.bitcast(FP8X4),
+                rhs_scale=scales,
+                start=True,
+                stop=True,
+            )
+
+        xg_w = held.tile([P, S], U32, name="xg_w", align_bytes=64)
+        xg_s = held.tile([P, S], U8, name="xg_s", align_bytes=64)
+        deal_words(0)
+        nc.vector.tensor_copy(out=xg_s[:], in_=xs[:].indirect(offs_sb[:]))
+        deal_scales(0)
+        half = S // 2
+        y_acc = [psum.tile([P, S], F32, name="acc") for t in range(PACK)]
+        for h in range(2):
+            cols = slice(h * half, (h + 1) * half)
+            nc.vector.tensor_copy(
+                out=xg_w[:, cols], in_=xw[:].bitcast(U32).indirect(offs_sb[:, h * half // 16 : (h + 1) * half // 16])
+            )
+            for t in range(PACK):
+                product(0, t, y_acc[t][:, cols], xg_w[:, cols], xg_s[:, cols])
+        deal_words(2)
+        deal_words(1)
+
+        yg = held.tile([P, PACK, S], F32, name="yg")
+        for t in range(PACK):
+            nc.scalar.copy(out=y_win[t][:, :S], in_=y_acc[t][:])
+        for t in range(PACK):
+            nc.scalar.activation(out=yg[:, t, :], in_=y_acc[t][:], func=ACT.Copy, scale=gn_sb[:, t : t + 1])
+
+        g3 = [ring.tile([P, S], F32, name="g3_%d" % t, bufs=1) for t in range(PACK)]
+        g4 = [ring.tile([P, S], F32, name="g4_%d" % t, bufs=1) for t in range(PACK)]
+        low = held.tile([P, PACK, S], F32, name="low")
+        z2_planes = held.tile([P, PACK, S], BF16, name="z2_planes")
+
+        def larger(t):
+            nc.vector.tensor_tensor(out=st_win[t][:, :S], in0=g3[t][:], in1=y_win[t][:, :S], op=ALU.max)
+
+        def smaller(t):
+            nc.vector.tensor_tensor(out=low[:, t, :], in0=g4[t][:], in1=st_win[t][:, :S], op=ALU.min)
+            nc.scalar.activation(out=z2_planes[:, t, :], in_=low[:, t, :], func=ACT.Copy, scale=gm_sb[:, t : t + 1])
+
+        for t in range(PACK):
+            nc.vector.tensor_copy(out=g3[t][:], in_=y_win[t][:].indirect(n3_sb[:]))
+            if t > 0:
+                larger(t - 1)
+        for t in range(PACK):
+            nc.vector.tensor_copy(out=g4[t][:], in_=st_win[t][:].indirect(n4_sb[:]))
+            if t == 0:
+                larger(PACK - 1)
+            else:
+                smaller(t - 1)
+        deal_scales(2)
+        smaller(PACK - 1)
+        deal_scales(1)
+        z2_bf = held.tile([P, S, PACK], BF16, name="z2_bf", align_bytes=64)
+        nc.scalar.copy(
+            out=z2_bf[:].rearrange("p (c i) t -> p c t i", i=4),
+            in_=z2_planes[:].rearrange("p t (c i) -> p c t i", i=4),
+        )
+
+        g1 = [ring.tile([P, S], F32, name="g1_%d" % t, bufs=1) for t in range(PACK)]
+        diff = [ring.tile([P, S], F32, name="diff_%d" % t, bufs=1) for t in range(PACK)]
+        sig1 = held.tile([P, PACK, S], F32, name="sig1")
+        z2_w = held.tile([P, S], U32, name="z2_w", align_bytes=64)
+        z2_s = held.tile([P, S], U8, name="z2_s", align_bytes=64)
+        b_plain = held.tile([P, PACK, S], F32, name="b_plain")
+
+        def difference(t):
+            nc.vector.tensor_tensor(out=diff[t][:], in0=y_win[t][:].indirect(n2_sb[:]), in1=g1[t][:], op=ALU.subtract)
+            nc.scalar.activation(out=sig1[:, t, :], in_=diff[t][:], func=ACT.Sigmoid, scale=-1.0)
+
+        for t in range(PACK):
+            nc.vector.tensor_copy(out=g1[t][:], in_=y_win[t][:].indirect(n1_sb[:]))
+            if t > 0:
+                difference(t - 1)
+            if t == 2:
+                nc.vector.quantize_mx(out=z2_w[:].bitcast(FP8X4), scales=z2_s[:], in_=z2_bf[:].rearrange("p c t -> p (c t)"))
+                b_acc = [psum.tile([P, S], F32, name="acc") for u in range(PACK)]
+                for u in range(PACK):
+                    product(2, u, b_acc[u][:], z2_w[:], z2_s[:])
+        difference(PACK - 1)
+        for t in range(PACK):
+            nc.scalar.copy(out=st_win[t][:, :S], in_=b_acc[t][:])
+            nc.scalar.copy(out=b_plain[:, t, :], in_=b_acc[t][:])
+
+        b_sum = [ring.tile([P, S], F32, name="b_sum%d" % t, bufs=1) for t in range(PACK)]
+        sig2 = held.tile([P, PACK, S], F32, name="sig2")
+
+        def gate(t):
+            nc.vector.tensor_tensor(out=b_sum[t][:], in0=st_win[t][:].indirect(n6_sb[:]), in1=b_plain[:, t, :], op=ALU.add)
+
+        z_bf = held.tile([P, S, PACK], BF16, name="z_bf", align_bytes=64)
+        z_w = held.tile([P, S], U32, name="z_w", align_bytes=64)
+        z_s = held.tile([P, S], U8, name="z_s", align_bytes=64)
+        gate(0)
+        nc.vector.tensor_tensor(
+            out=z_bf[:].rearrange("p (c i) t -> p c t i", i=2),
+            in0=sig1[:].rearrange("p t (c i) -> p c t i", i=2),
+            in1=yg[:].rearrange("p t (c i) -> p c t i", i=2),
+            op=ALU.mult,
+        )
+        gate(1)
+        nc.vector.quantize_mx(out=z_w[:].bitcast(FP8X4), scales=z_s[:], in_=z_bf[:].rearrange("p c t -> p (c t)"))
+        a_acc = [psum.tile([P, S], F32, name="acc") for t in range(PACK)]
+        for t in range(PACK):
+            product(1, t, a_acc[t][:], z_w[:], z_s[:])
+        gate(2)
+        gate(3)
+        a_win = [held.tile([P, S], F32, name="a_win%d" % t) for t in range(PACK)]
+        a_plain = held.tile([P, PACK, S], F32, name="a_plain")
+        for t in range(2):
+            nc.scalar.activation(out=sig2[:, t, :], in_=b_sum[t][:], func=ACT.Sigmoid)
+        for t in range(PACK):
+            nc.scalar.copy(out=a_win[t][:], in_=a_acc[t][:])
+            nc.scalar.copy(out=a_plain[:, t, :], in_=a_acc[t][:])
+        for t in range(2, PACK):
+            nc.scalar.activation(out=sig2[:, t, :], in_=b_sum[t][:], func=ACT.Sigmoid)
+
+        out_w = held.tile([P, S], U32, name="out_w", align_bytes=64)
+        out_s = held.tile([P, S], U8, name="out_s", align_bytes=64)
+        out_rows = out_0.rearrange("(p t) c -> p t c", t=PACK)
+        out_words = out_1[0].rearrange("p c r -> p (c r)").bitcast(I32)
+        pending = None
+
+        def hand_on(c0, width, rounded):
+            cols = slice(c0, c0 + width)
+            nc.vector.quantize_mx(out=out_w[:, cols].bitcast(FP8X4), scales=out_s[:, cols], in_=rounded[:].rearrange("p c t -> p (c t)"))
+            nc.sync.dma_start(out=out_words[:, cols], in_=out_w[:, cols].bitcast(I32))
+
+        for k, (c0, width) in enumerate(OUT_CHUNKS):
+            cols = slice(c0, c0 + width)
+            a_sum = held.tile([P, PACK, width], F32, name="a_sum%d" % k)
+            res = held.tile([P, PACK, width], F32, name="res%d" % k)
+            rounded = held.tile([P, width, PACK], BF16, name="rounded%d" % k, align_bytes=64)
+            for t in range(PACK):
+                nc.vector.tensor_tensor(
+                    out=a_sum[:, t, :],
+                    in0=a_win[t][:].indirect(n5_sb[:, c0 // 16 : (c0 + width) // 16]),
+                    in1=a_plain[:, t, cols],
+                    op=ALU.add,
+                )
+            if pending is not None:
+                hand_on(*pending)
+            nc.vector.tensor_tensor(out=res[:], in0=a_sum[:], in1=sig2[:, :, cols], op=ALU.mult)
+            nc.sync.dma_start(out=out_rows[:, :, cols], in_=res[:])
+            dst = rounded[:].rearrange("p (c i) t -> p c t i", i=2)
+            src = res[:].rearrange("p t (c i) -> p c t i", i=2)
+            if k == len(OUT_CHUNKS) - 1:
+                nc.vector.tensor_copy(out=dst, in_=src)
+            else:
+                nc.scalar.copy(out=dst, in_=src)
+            pending = (c0, width, rounded)
+        hand_on(*pending)
+        for q in range(4):
+            queue = nc.scalar if q % 2 else nc.sync
+            queue.dma_start(out=out_2[0, 4 * q : 4 * q + 4, :].bitcast(I32), in_=out_s[32 * q : 32 * q + 4, :].bitcast(I32))

@@ -1,6 +1,7 @@
 from contextlib import ExitStack
 
 import concourse.mybir as mybir
+from concourse.masks import make_identity
 
 K, T, S, N, H = 512, 2048, 512, 512, 512
 FLOPS = 3 * 2 * 512 * 512 * 512
@@ -18,6 +19,7 @@ ACT = mybir.ActivationFunctionType
 
 P = 128
 PACK = 4
+HALF = S // 2
 OUT_CHUNKS = ((0, 256), (256, 128), (384, 128))
 
 
@@ -33,34 +35,33 @@ def tile_picked_forktriebcmphopmn_none_po_kernel(
     nc = tc.nc
     with ExitStack() as ctx:
         held = ctx.enter_context(tc.tile_pool(name="held", bufs=1))
-        ring = ctx.enter_context(tc.tile_pool(name="ring", bufs=2))
         psum = ctx.enter_context(tc.psum_pool(name="psum", bufs=8))
 
-        def list_tile(name):
-            return held.tile([P, S // 16], U16, name=name)
+        def four(name, shape, dtype):
+            return [held.tile(shape, dtype, name="%s%d" % (name, t), align_bytes=64) for t in range(PACK)]
 
-        offs_sb = list_tile("offs_sb")
-        n_sb = [list_tile("n%d_sb" % i) for i in range(1, 7)]
-        n1_sb, n2_sb, n3_sb, n4_sb, n5_sb, n6_sb = n_sb
+        offs_sb = held.tile([P, S // 16], U16, name="offs_sb")
+        n1_sb, n2_sb, n3_sb, n4_sb, n5_sb, n6_sb = [held.tile([P, S // 16], U16, name="n%d_sb" % i) for i in range(1, 7)]
 
         xw = held.tile([P, T], I32, name="xw", align_bytes=64)
         xs = held.tile([P, T], U8, name="xs", align_bytes=64)
         raw_w = [held.tile([P, 2 * H], U8, name="raw_w%d" % i, align_bytes=64) for i in range(3)]
         raw_s = [held.tile([P, H], U8, name="raw_s%d" % i, align_bytes=64) for i in range(3)]
-        deal_w = [held.tile([P, 2 * H], U8, name="deal_w%d" % i, align_bytes=64) for i in range(3)]
-        deal_s = [held.tile([P, H], U8, name="deal_s%d" % i, align_bytes=64) for i in range(3)]
+        deal_w = {}
+        deal_s = {}
         gn_sb = held.tile([P, PACK], F32, name="gn_sb")
         gm_sb = held.tile([P, PACK], F32, name="gm_sb")
-        y_win = [held.tile([P, 2 * S], F32, name="y_win%d" % t) for t in range(PACK)]
-        st_win = [held.tile([P, 2 * S], F32, name="st_win%d" % t) for t in range(PACK)]
+        y_win = four("y_win", [P, 2 * S], F32)
+        st_win = four("st_win", [P, 2 * S], F32)
 
-        nc.vector.memset(xs[:].bitcast(I32), 0)
+        nc.vector.memset(xs[:, : T // 2].bitcast(I32), 0)
+        nc.gpsimd.memset(xs[:, T // 2 :].bitcast(I32), 0)
         nc.vector.memset(raw_s[0][:].bitcast(I32), 0)
-        nc.vector.memset(raw_s[2][:].bitcast(I32), 0)
         nc.vector.memset(raw_s[1][:].bitcast(I32), 0)
-        for t in range(PACK):
-            nc.vector.memset(y_win[t][:, S:], 0.0)
-            nc.gpsimd.memset(st_win[t][:, S:], 0.0)
+        nc.vector.memset(raw_s[2][:].bitcast(I32), 0)
+
+        ident = held.tile([P, P], F32, name="ident")
+        make_identity(nc, ident[:])
 
         w_words = (w1_words, w2_words, w3_words)
         w_scales = (w1_scales, w2_scales, w3_scales)
@@ -69,31 +70,33 @@ def tile_picked_forktriebcmphopmn_none_po_kernel(
             nc.sync.dma_start(out=raw_w[i][:].bitcast(I32), in_=w_words[i][0].bitcast(I32))
 
         nc.sync.dma_start(offs_sb[:], offs)
-        nc.sync.dma_start(out=xw[:], in_=x_words[0].rearrange("p c r -> p (c r)").bitcast(I32))
         load_words(0)
+        nc.sync.dma_start(n3_sb[:], n3)
         load_scale_rows(nc.sync, xs, x_scales)
+        nc.sync.dma_start(out=xw[:], in_=x_words[0].rearrange("p c r -> p (c r)").bitcast(I32))
         load_scale_rows(nc.sync, raw_s[0], w_scales[0])
         load_words(2)
-        load_words(1)
-        nc.sync.dma_start(n3_sb[:], n3)
         nc.sync.dma_start(n4_sb[:], n4)
         nc.sync.dma_start(out=gm_sb[:], in_=gm.rearrange("(p t) o -> p (t o)", t=PACK))
         nc.sync.dma_start(out=gn_sb[:], in_=gn.rearrange("(p t) o -> p (t o)", t=PACK))
         load_scale_rows(nc.sync, raw_s[2], w_scales[2])
-        load_scale_rows(nc.sync, raw_s[1], w_scales[1])
         nc.sync.dma_start(n1_sb[:], n1)
         nc.sync.dma_start(n2_sb[:], n2)
+        load_words(1)
+        load_scale_rows(nc.sync, raw_s[1], w_scales[1])
         nc.sync.dma_start(n6_sb[:], n6)
         nc.sync.dma_start(n5_sb[:], n5)
 
-        def deal_words(i):
-            nc.vector.tensor_copy(
+        def deal_words(engine, i):
+            deal_w[i] = held.tile([P, 2 * H], U8, name="deal_w%d" % i, tag="deal_w%d" % min(i, 1), align_bytes=64)
+            engine.tensor_copy(
                 out=deal_w[i][:].rearrange("p (t m b) -> p t m b", t=PACK, b=2),
                 in_=raw_w[i][:].rearrange("p (m t b) -> p t m b", t=PACK, b=2),
             )
 
-        def deal_scales(i):
-            nc.vector.tensor_copy(
+        def deal_scales(engine, i):
+            deal_s[i] = held.tile([P, H], U8, name="deal_s%d" % i, tag="deal_s%d" % min(i, 1), align_bytes=64)
+            engine.tensor_copy(
                 out=deal_s[i][:].rearrange("p (t m) -> p t m", t=PACK),
                 in_=raw_s[i][:].rearrange("p (m t) -> p t m", t=PACK),
             )
@@ -109,153 +112,222 @@ def tile_picked_forktriebcmphopmn_none_po_kernel(
                 stop=True,
             )
 
-        xg_w = held.tile([P, S], U32, name="xg_w", align_bytes=64)
-        xg_s = held.tile([P, S], U8, name="xg_s", align_bytes=64)
-        deal_words(0)
-        nc.vector.tensor_copy(out=xg_s[:], in_=xs[:].indirect(offs_sb[:]))
-        deal_scales(0)
-        half = S // 2
-        y_acc = [psum.tile([P, S], F32, name="acc") for t in range(PACK)]
-        for h in range(2):
-            cols = slice(h * half, (h + 1) * half)
-            nc.vector.tensor_copy(
-                out=xg_w[:, cols], in_=xw[:].bitcast(U32).indirect(offs_sb[:, h * half // 16 : (h + 1) * half // 16])
+        def interleave(rows, planes, cols):
+            nc.scalar.copy(
+                out=rows[:].rearrange("p (c i) t -> p c t i", i=4),
+                in_=planes[:, :, cols].rearrange("p t (c i) -> p c t i", i=4),
             )
-            for t in range(PACK):
-                product(0, t, y_acc[t][:, cols], xg_w[:, cols], xg_s[:, cols])
-        deal_words(2)
-        deal_words(1)
 
+        def quantize(codes, scales, rows):
+            nc.vector.quantize_mx(out=codes.bitcast(FP8X4), scales=scales, in_=rows[:].rearrange("p c t -> p (c t)"))
+
+        halves = [slice(h * HALF, (h + 1) * HALF) for h in range(2)]
+
+        xg_w = []
+        xg_s = held.tile([P, S], U8, name="xg_s", align_bytes=64)
+        deal_words(nc.vector, 0)
+        nc.vector.tensor_copy(out=xg_s[:], in_=xs[:].indirect(offs_sb[:]))
+        deal_scales(nc.vector, 0)
+        for h, cols in enumerate(halves):
+            xg_w.append(held.tile([P, HALF], U32, name="xg_w%d" % h, tag=("xg_w0", "raw_s0")[h], align_bytes=64))
+            nc.vector.tensor_copy(
+                out=xg_w[h][:], in_=xw[:].bitcast(U32).indirect(offs_sb[:, h * HALF // 16 : (h + 1) * HALF // 16])
+            )
+        deal_words(nc.vector, 2)
+        deal_scales(nc.vector, 2)
+        y_acc = [[psum.tile([P, HALF], F32, name="acc") for h in range(2)] for t in range(PACK)]
         yg = held.tile([P, PACK, S], F32, name="yg")
         for t in range(PACK):
-            nc.scalar.copy(out=y_win[t][:, :S], in_=y_acc[t][:])
+            for h, cols in enumerate(halves):
+                product(0, t, y_acc[t][h][:], xg_w[h][:], xg_s[:, cols])
+                nc.scalar.copy(out=y_win[t][:, cols], in_=y_acc[t][h][:])
         for t in range(PACK):
-            nc.scalar.activation(out=yg[:, t, :], in_=y_acc[t][:], func=ACT.Copy, scale=gn_sb[:, t : t + 1])
+            for h, cols in enumerate(halves):
+                nc.scalar.activation(out=yg[:, t, cols], in_=y_acc[t][h][:], func=ACT.Copy, scale=gn_sb[:, t : t + 1])
 
-        g3 = [ring.tile([P, S], F32, name="g3_%d" % t, bufs=1) for t in range(PACK)]
-        g4 = [ring.tile([P, S], F32, name="g4_%d" % t, bufs=1) for t in range(PACK)]
-        low = held.tile([P, PACK, S], F32, name="low")
-        z2_planes = held.tile([P, PACK, S], BF16, name="z2_planes")
+        def fetched(name, slot):
+            return held.tile([P, S], F32, name=name, tag="fetched%d" % slot, align_bytes=64)
+
+        g3, g4, st_turned = [], [], []
+        z2_planes = held.tile([P, PACK, S], BF16, name="z2_planes", tag="planes")
+        minus_gm = held.tile([P, PACK], F32, name="minus_gm")
+        nc.scalar.activation(out=minus_gm[:], in_=gm_sb[:], func=ACT.Copy, scale=-1.0)
+
+        def turn(bank, src, first, last):
+            for k in range(PACK):
+                nc.tensor.matmul(
+                    out=bank[:, P * k : P * (k + 1)], lhsT=src[:, P * k : P * (k + 1)], rhs=ident[:], is_transpose=True,
+                    start=first and k == 0, stop=last and k == PACK - 1,
+                )
 
         def larger(t):
             nc.vector.tensor_tensor(out=st_win[t][:, :S], in0=g3[t][:], in1=y_win[t][:, :S], op=ALU.max)
+            bank = psum.tile([P, S], F32, name="acc")
+            turn(bank, st_win[t], True, True)
+            st_turned.append(held.tile([P, S], F32, name="st_turned%d" % t))
+            nc.scalar.activation(out=st_turned[t][:], in_=bank[:], func=ACT.Copy, scale=-1.0)
 
         def smaller(t):
-            nc.vector.tensor_tensor(out=low[:, t, :], in0=g4[t][:], in1=st_win[t][:, :S], op=ALU.min)
-            nc.scalar.activation(out=z2_planes[:, t, :], in_=low[:, t, :], func=ACT.Copy, scale=gm_sb[:, t : t + 1])
+            gap = psum.tile([P, S], F32, name="acc")
+            turn(gap, st_win[t], True, False)
+            turn(gap, g4[t], False, True)
+            excess = held.tile([P, S], F32, name="excess%d" % t)
+            nc.scalar.activation(out=excess[:], in_=gap[:], func=ACT.Relu)
+            return excess
+
+        def scaled(t, excess):
+            low = psum.tile([P, S], F32, name="acc")
+            turn(low, st_turned[t], True, False)
+            turn(low, excess, False, True)
+            nc.scalar.activation(out=z2_planes[:, t, :], in_=low[:], func=ACT.Copy, scale=minus_gm[:, t : t + 1])
 
         for t in range(PACK):
+            g3.append(fetched("g3_%d" % t, t))
             nc.vector.tensor_copy(out=g3[t][:], in_=y_win[t][:].indirect(n3_sb[:]))
             if t > 0:
                 larger(t - 1)
+        excess = []
         for t in range(PACK):
-            nc.vector.tensor_copy(out=g4[t][:], in_=st_win[t][:].indirect(n4_sb[:]))
+            g4.append(fetched("g4_%d" % t, (6, 7, 8, 12)[t]))
+            nc.vector.tensor_scalar(
+                out=g4[t][:], in0=st_win[t][:].indirect(n4_sb[:]), scalar1=-1.0, scalar2=0.0, op0=ALU.mult, op1=ALU.add
+            )
             if t == 0:
                 larger(PACK - 1)
-            else:
-                smaller(t - 1)
-        deal_scales(2)
-        smaller(PACK - 1)
-        deal_scales(1)
-        z2_bf = held.tile([P, S, PACK], BF16, name="z2_bf", align_bytes=64)
-        nc.scalar.copy(
-            out=z2_bf[:].rearrange("p (c i) t -> p c t i", i=4),
-            in_=z2_planes[:].rearrange("p t (c i) -> p c t i", i=4),
-        )
+            excess.append(smaller(t))
+            if t > 0:
+                scaled(t - 1, excess[t - 1])
+        scaled(PACK - 1, excess[PACK - 1])
 
-        g1 = [ring.tile([P, S], F32, name="g1_%d" % t, bufs=1) for t in range(PACK)]
-        diff = [ring.tile([P, S], F32, name="diff_%d" % t, bufs=1) for t in range(PACK)]
-        sig1 = held.tile([P, PACK, S], F32, name="sig1")
+        z2_bf = [held.tile([P, HALF, PACK], BF16, name="z2_bf%d" % h, tag="fetched%d" % (4 + h), align_bytes=64) for h in range(2)]
         z2_w = held.tile([P, S], U32, name="z2_w", align_bytes=64)
         z2_s = held.tile([P, S], U8, name="z2_s", align_bytes=64)
-        b_plain = held.tile([P, PACK, S], F32, name="b_plain")
+        for h, cols in enumerate(halves):
+            interleave(z2_bf[h], z2_planes, cols)
+
+        g1 = []
+        diff = []
+        sig1 = held.tile([P, PACK, S], F32, name="sig1", tag="planes")
+        b_acc = [psum.tile([P, S], F32, name="acc") for t in range(PACK)]
+        b_plain = four("b_plain", [P, S], F32)
 
         def difference(t):
+            diff.append(fetched("diff%d" % t, (9, 10, 11, 5)[t]))
             nc.vector.tensor_tensor(out=diff[t][:], in0=y_win[t][:].indirect(n2_sb[:]), in1=g1[t][:], op=ALU.subtract)
             nc.scalar.activation(out=sig1[:, t, :], in_=diff[t][:], func=ACT.Sigmoid, scale=-1.0)
 
+        def b_half(h):
+            cols = halves[h]
+            quantize(z2_w[:, cols], z2_s[:, cols], z2_bf[h])
+            for t in range(PACK):
+                product(2, t, b_acc[t][:, cols], z2_w[:, cols], z2_s[:, cols])
+
         for t in range(PACK):
+            if t == PACK - 1:
+                b_half(0)
+            g1.append(fetched("g1_%d" % t, (3, 2, 1, 4)[t]))
             nc.vector.tensor_copy(out=g1[t][:], in_=y_win[t][:].indirect(n1_sb[:]))
             if t > 0:
                 difference(t - 1)
-            if t == 2:
-                nc.vector.quantize_mx(out=z2_w[:].bitcast(FP8X4), scales=z2_s[:], in_=z2_bf[:].rearrange("p c t -> p (c t)"))
-                b_acc = [psum.tile([P, S], F32, name="acc") for u in range(PACK)]
-                for u in range(PACK):
-                    product(2, u, b_acc[u][:], z2_w[:], z2_s[:])
+        b_half(1)
         difference(PACK - 1)
+        deal_words(nc.vector, 1)
+        deal_scales(nc.vector, 1)
         for t in range(PACK):
             nc.scalar.copy(out=st_win[t][:, :S], in_=b_acc[t][:])
-            nc.scalar.copy(out=b_plain[:, t, :], in_=b_acc[t][:])
+            if t == 0:
+                nc.scalar.copy(out=b_plain[t][:], in_=b_acc[t][:])
+            else:
+                nc.sync.dma_start(out=b_plain[t][:], in_=st_win[t][:, :S])
 
-        b_sum = [ring.tile([P, S], F32, name="b_sum%d" % t, bufs=1) for t in range(PACK)]
-        sig2 = held.tile([P, PACK, S], F32, name="sig2")
-
-        def gate(t):
-            nc.vector.tensor_tensor(out=b_sum[t][:], in0=st_win[t][:].indirect(n6_sb[:]), in1=b_plain[:, t, :], op=ALU.add)
-
-        z_bf = held.tile([P, S, PACK], BF16, name="z_bf", align_bytes=64)
+        z_bf = [held.tile([P, HALF, PACK], BF16, name="z_bf%d" % h, tag="fetched%d" % (7 + h), align_bytes=64) for h in range(2)]
         z_w = held.tile([P, S], U32, name="z_w", align_bytes=64)
         z_s = held.tile([P, S], U8, name="z_s", align_bytes=64)
+        sig2 = held.tile([P, PACK, S], F32, name="sig2")
+        a_acc = [[psum.tile([P, HALF], F32, name="acc") for t in range(PACK)] for h in range(2)]
+        a_win = four("a_win", [P, S], F32)
+        a_plain = four("a_plain", [P, S], F32)
+
+        def gate(t):
+            b_sum = fetched("b_sum%d" % t, (0, 6, 7, 8)[t])
+            nc.vector.tensor_tensor(out=b_sum[:], in0=st_win[t][:].indirect(n6_sb[:]), in1=b_plain[t][:], op=ALU.add)
+            nc.scalar.activation(out=sig2[:, t, :], in_=b_sum[:], func=ACT.Sigmoid)
+
+        def z_half(h):
+            nc.vector.tensor_tensor(
+                out=z_bf[h][:].rearrange("p (c i) t -> p c t i", i=2),
+                in0=sig1[:, :, halves[h]].rearrange("p t (c i) -> p c t i", i=2),
+                in1=yg[:, :, halves[h]].rearrange("p t (c i) -> p c t i", i=2),
+                op=ALU.mult,
+            )
+
+        def a_half(h):
+            cols = halves[h]
+            quantize(z_w[:, cols], z_s[:, cols], z_bf[h])
+            for t in range(PACK):
+                product(1, t, a_acc[h][t][:], z_w[:, cols], z_s[:, cols])
+
+        z_half(0)
+        z_half(1)
         gate(0)
-        nc.vector.tensor_tensor(
-            out=z_bf[:].rearrange("p (c i) t -> p c t i", i=2),
-            in0=sig1[:].rearrange("p t (c i) -> p c t i", i=2),
-            in1=yg[:].rearrange("p t (c i) -> p c t i", i=2),
-            op=ALU.mult,
-        )
+        a_half(0)
+        a_half(1)
         gate(1)
-        nc.vector.quantize_mx(out=z_w[:].bitcast(FP8X4), scales=z_s[:], in_=z_bf[:].rearrange("p c t -> p (c t)"))
-        a_acc = [psum.tile([P, S], F32, name="acc") for t in range(PACK)]
         for t in range(PACK):
-            product(1, t, a_acc[t][:], z_w[:], z_s[:])
+            nc.scalar.copy(out=a_win[t][:, halves[0]], in_=a_acc[0][t][:])
+            nc.scalar.copy(out=a_win[t][:, halves[1]], in_=a_acc[1][t][:])
+            nc.scalar.copy(out=a_plain[t][:, halves[0]], in_=a_acc[0][t][:])
+            nc.sync.dma_start(out=a_plain[t][:, halves[1]], in_=a_win[t][:, halves[1]])
         gate(2)
         gate(3)
-        a_win = [held.tile([P, S], F32, name="a_win%d" % t) for t in range(PACK)]
-        a_plain = held.tile([P, PACK, S], F32, name="a_plain")
-        for t in range(2):
-            nc.scalar.activation(out=sig2[:, t, :], in_=b_sum[t][:], func=ACT.Sigmoid)
-        for t in range(PACK):
-            nc.scalar.copy(out=a_win[t][:], in_=a_acc[t][:])
-            nc.scalar.copy(out=a_plain[:, t, :], in_=a_acc[t][:])
-        for t in range(2, PACK):
-            nc.scalar.activation(out=sig2[:, t, :], in_=b_sum[t][:], func=ACT.Sigmoid)
 
         out_w = held.tile([P, S], U32, name="out_w", align_bytes=64)
         out_s = held.tile([P, S], U8, name="out_s", align_bytes=64)
         out_rows = out_0.rearrange("(p t) c -> p t c", t=PACK)
         out_words = out_1[0].rearrange("p c r -> p (c r)").bitcast(I32)
-        pending = None
+        a_sum = {}
+        rounded = {}
 
-        def hand_on(c0, width, rounded):
-            cols = slice(c0, c0 + width)
-            nc.vector.quantize_mx(out=out_w[:, cols].bitcast(FP8X4), scales=out_s[:, cols], in_=rounded[:].rearrange("p c t -> p (c t)"))
-            nc.sync.dma_start(out=out_words[:, cols], in_=out_w[:, cols].bitcast(I32))
-
-        for k, (c0, width) in enumerate(OUT_CHUNKS):
-            cols = slice(c0, c0 + width)
-            a_sum = held.tile([P, PACK, width], F32, name="a_sum%d" % k)
-            res = held.tile([P, PACK, width], F32, name="res%d" % k)
-            rounded = held.tile([P, width, PACK], BF16, name="rounded%d" % k, align_bytes=64)
+        def fetch(k):
+            c0, width = OUT_CHUNKS[k]
+            a_sum[k] = held.tile([P, PACK, width], F32, name="a_sum%d" % k, tag="a_sum%d" % (k % 2))
             for t in range(PACK):
                 nc.vector.tensor_tensor(
-                    out=a_sum[:, t, :],
+                    out=a_sum[k][:, t, :],
                     in0=a_win[t][:].indirect(n5_sb[:, c0 // 16 : (c0 + width) // 16]),
-                    in1=a_plain[:, t, cols],
+                    in1=a_plain[t][:, c0 : c0 + width],
                     op=ALU.add,
                 )
-            if pending is not None:
-                hand_on(*pending)
-            nc.vector.tensor_tensor(out=res[:], in0=a_sum[:], in1=sig2[:, :, cols], op=ALU.mult)
+
+        def combine(k):
+            c0, width = OUT_CHUNKS[k]
+            cols = slice(c0, c0 + width)
+            res = held.tile([P, PACK, width], F32, name="res%d" % k)
+            rounded[k] = held.tile([P, width, PACK], BF16, name="rounded%d" % k, align_bytes=64)
+            nc.vector.tensor_tensor(out=res[:], in0=a_sum[k][:], in1=sig2[:, :, cols], op=ALU.mult)
             nc.sync.dma_start(out=out_rows[:, :, cols], in_=res[:])
-            dst = rounded[:].rearrange("p (c i) t -> p c t i", i=2)
+            dst = rounded[k][:].rearrange("p (c i) t -> p c t i", i=2)
             src = res[:].rearrange("p t (c i) -> p c t i", i=2)
             if k == len(OUT_CHUNKS) - 1:
                 nc.vector.tensor_copy(out=dst, in_=src)
             else:
                 nc.scalar.copy(out=dst, in_=src)
-            pending = (c0, width, rounded)
-        hand_on(*pending)
+
+        def hand_on(k):
+            c0, width = OUT_CHUNKS[k]
+            cols = slice(c0, c0 + width)
+            quantize(out_w[:, cols], out_s[:, cols], rounded[k])
+            nc.sync.dma_start(out=out_words[:, cols], in_=out_w[:, cols].bitcast(I32))
+
+        fetch(0)
+        combine(0)
+        fetch(1)
+        combine(1)
+        hand_on(0)
+        fetch(2)
+        combine(2)
+        hand_on(1)
+        hand_on(2)
         for q in range(4):
             queue = nc.scalar if q % 2 else nc.sync
             queue.dma_start(out=out_2[0, 4 * q : 4 * q + 4, :].bitcast(I32), in_=out_s[32 * q : 32 * q + 4, :].bitcast(I32))

@@ -3,7 +3,9 @@ from contextlib import ExitStack
 import concourse.mybir as mybir
 from concourse.masks import make_identity
 
-K, T, S, N, H = 512, 2048, 512, 512, 512
+T = 2048
+S = 512
+H = 512
 FLOPS = 3 * 2 * 512 * 512 * 512
 
 F32 = mybir.dt.float32
@@ -18,14 +20,20 @@ ALU = mybir.AluOpType
 ACT = mybir.ActivationFunctionType
 
 P = 128
-PACK = 4
+PLANES = 4
+QUADRANTS = 4
+BANKS = 8
 HALF = S // 2
-OUT_CHUNKS = ((0, 256), (256, 128), (384, 128))
+STRIPE = 16
+W1, W2, W3 = 0, 1, 2
+OUT_RANGES = ((0, 256), (256, 128), (384, 128))
 
 
-def load_scale_rows(queue, plane, rows):
-    for q in range(4):
-        queue.dma_start(out=plane[32 * q : 32 * q + 4, :].bitcast(I32), in_=rows[0, 4 * q : 4 * q + 4, :].bitcast(I32))
+def load_scale_rows(nc, scale_tile, rows):
+    for q in range(QUADRANTS):
+        nc.sync.dma_start(
+            out=scale_tile[32 * q : 32 * q + 4, :].bitcast(I32), in_=rows[0, 4 * q : 4 * q + 4, :].bitcast(I32)
+        )
 
 
 def tile_picked_forktriebcmphopmn_none_po_kernel(
@@ -35,30 +43,45 @@ def tile_picked_forktriebcmphopmn_none_po_kernel(
     nc = tc.nc
     with ExitStack() as ctx:
         held = ctx.enter_context(tc.tile_pool(name="held", bufs=1))
-        psum = ctx.enter_context(tc.psum_pool(name="psum", bufs=8))
+        psum = ctx.enter_context(tc.psum_pool(name="psum", bufs=1))
+        halves = [slice(h * HALF, (h + 1) * HALF) for h in range(2)]
+        last = PLANES - 1
 
-        def four(name, shape, dtype):
-            return [held.tile(shape, dtype, name="%s%d" % (name, t), align_bytes=64) for t in range(PACK)]
+        def bank(number, width):
+            return psum.tile([P, width], F32, name="bank%d" % number)
 
-        offs_sb = held.tile([P, S // 16], U16, name="offs_sb")
-        n1_sb, n2_sb, n3_sb, n4_sb, n5_sb, n6_sb = [held.tile([P, S // 16], U16, name="n%d_sb" % i) for i in range(1, 7)]
+        banks_taken = []
 
-        xw = held.tile([P, T], I32, name="xw", align_bytes=64)
-        xs = held.tile([P, T], U8, name="xs", align_bytes=64)
-        raw_w = [held.tile([P, 2 * H], U8, name="raw_w%d" % i, align_bytes=64) for i in range(3)]
-        raw_s = [held.tile([P, H], U8, name="raw_s%d" % i, align_bytes=64) for i in range(3)]
-        deal_w = {}
-        deal_s = {}
-        gn_sb = held.tile([P, PACK], F32, name="gn_sb")
-        gm_sb = held.tile([P, PACK], F32, name="gm_sb")
-        y_win = four("y_win", [P, 2 * S], F32)
-        st_win = four("st_win", [P, 2 * S], F32)
+        def next_bank(width):
+            banks_taken.append(width)
+            return bank((PLANES + len(banks_taken) - 1) % BANKS, width)
 
-        nc.vector.memset(xs[:, : T // 2].bitcast(I32), 0)
-        nc.gpsimd.memset(xs[:, T // 2 :].bitcast(I32), 0)
-        nc.vector.memset(raw_s[0][:].bitcast(I32), 0)
-        nc.vector.memset(raw_s[1][:].bitcast(I32), 0)
-        nc.vector.memset(raw_s[2][:].bitcast(I32), 0)
+        def per_plane(name, width):
+            return [held.tile([P, width], F32, name="%s%d" % (name, t), align_bytes=64) for t in range(PLANES)]
+
+        def plane_in(buffer, name):
+            return held.tile([P, S], F32, name=name, tag=buffer, align_bytes=64)
+
+        def entries(list_tile, first, count):
+            return list_tile[:, first // STRIPE : (first + count) // STRIPE]
+
+        offs_sb = held.tile([P, S // STRIPE], U16, name="offs_sb")
+        n1_sb, n2_sb, n3_sb, n4_sb, n5_sb, n6_sb = [
+            held.tile([P, S // STRIPE], U16, name="n%d_sb" % i) for i in range(1, 7)
+        ]
+        x_table = held.tile([P, T], I32, name="x_table", align_bytes=64)
+        x_table_scales = held.tile([P, T], U8, name="x_table_scales", align_bytes=64)
+        raw_words = [held.tile([P, 2 * H], U8, name="raw_words%d" % w, align_bytes=64) for w in (W1, W2, W3)]
+        raw_scales = [held.tile([P, H], U8, name="raw_scales%d" % w, align_bytes=64) for w in (W1, W2, W3)]
+        gn_sb = held.tile([P, PLANES], F32, name="gn_sb")
+        gm_sb = held.tile([P, PLANES], F32, name="gm_sb")
+        y_win = per_plane("y_win", 2 * S)
+        st_win = per_plane("st_win", 2 * S)
+
+        nc.vector.memset(x_table_scales[:, : T // 2].bitcast(I32), 0)
+        nc.gpsimd.memset(x_table_scales[:, T // 2 :].bitcast(I32), 0)
+        for w in (W1, W2, W3):
+            nc.vector.memset(raw_scales[w][:].bitcast(I32), 0)
 
         ident = held.tile([P, P], F32, name="ident")
         make_identity(nc, ident[:])
@@ -66,268 +89,254 @@ def tile_picked_forktriebcmphopmn_none_po_kernel(
         w_words = (w1_words, w2_words, w3_words)
         w_scales = (w1_scales, w2_scales, w3_scales)
 
-        def load_words(i):
-            nc.sync.dma_start(out=raw_w[i][:].bitcast(I32), in_=w_words[i][0].bitcast(I32))
+        def load_words(w):
+            nc.sync.dma_start(out=raw_words[w][:].bitcast(I32), in_=w_words[w][0].bitcast(I32))
 
         nc.sync.dma_start(offs_sb[:], offs)
-        load_words(0)
+        load_words(W1)
         nc.sync.dma_start(n3_sb[:], n3)
-        load_scale_rows(nc.sync, xs, x_scales)
-        nc.sync.dma_start(out=xw[:], in_=x_words[0].rearrange("p c r -> p (c r)").bitcast(I32))
-        load_scale_rows(nc.sync, raw_s[0], w_scales[0])
-        load_words(2)
+        load_scale_rows(nc, x_table_scales, x_scales)
+        nc.sync.dma_start(out=x_table[:], in_=x_words[0].rearrange("p c r -> p (c r)").bitcast(I32))
+        load_scale_rows(nc, raw_scales[W1], w_scales[W1])
+        load_words(W3)
         nc.sync.dma_start(n4_sb[:], n4)
-        nc.sync.dma_start(out=gm_sb[:], in_=gm.rearrange("(p t) o -> p (t o)", t=PACK))
-        nc.sync.dma_start(out=gn_sb[:], in_=gn.rearrange("(p t) o -> p (t o)", t=PACK))
-        load_scale_rows(nc.sync, raw_s[2], w_scales[2])
+        nc.sync.dma_start(out=gm_sb[:], in_=gm.rearrange("(p t) o -> p (t o)", t=PLANES))
+        nc.sync.dma_start(out=gn_sb[:], in_=gn.rearrange("(p t) o -> p (t o)", t=PLANES))
+        load_scale_rows(nc, raw_scales[W3], w_scales[W3])
         nc.sync.dma_start(n1_sb[:], n1)
         nc.sync.dma_start(n2_sb[:], n2)
-        load_words(1)
-        load_scale_rows(nc.sync, raw_s[1], w_scales[1])
+        load_words(W2)
+        load_scale_rows(nc, raw_scales[W2], w_scales[W2])
         nc.sync.dma_start(n6_sb[:], n6)
         nc.sync.dma_start(n5_sb[:], n5)
 
-        def deal_words(engine, i):
-            deal_w[i] = held.tile([P, 2 * H], U8, name="deal_w%d" % i, tag="deal_w%d" % min(i, 1), align_bytes=64)
-            engine.tensor_copy(
-                out=deal_w[i][:].rearrange("p (t m b) -> p t m b", t=PACK, b=2),
-                in_=raw_w[i][:].rearrange("p (m t b) -> p t m b", t=PACK, b=2),
+        dealt_words = {}
+        dealt_scales = {}
+
+        def deal_words(w, buffer):
+            dealt_words[w] = held.tile([P, 2 * H], U8, name="dealt_words%d" % w, tag=buffer, align_bytes=64)
+            nc.vector.tensor_copy(
+                out=dealt_words[w][:].rearrange("p (t m b) -> p t m b", t=PLANES, b=2),
+                in_=raw_words[w][:].rearrange("p (m t b) -> p t m b", t=PLANES, b=2),
             )
 
-        def deal_scales(engine, i):
-            deal_s[i] = held.tile([P, H], U8, name="deal_s%d" % i, tag="deal_s%d" % min(i, 1), align_bytes=64)
-            engine.tensor_copy(
-                out=deal_s[i][:].rearrange("p (t m) -> p t m", t=PACK),
-                in_=raw_s[i][:].rearrange("p (m t) -> p t m", t=PACK),
+        def deal_scales(w, buffer):
+            dealt_scales[w] = held.tile([P, H], U8, name="dealt_scales%d" % w, tag=buffer, align_bytes=64)
+            nc.vector.tensor_copy(
+                out=dealt_scales[w][:].rearrange("p (t m) -> p t m", t=PLANES),
+                in_=raw_scales[w][:].rearrange("p (m t) -> p t m", t=PLANES),
             )
 
-        def product(i, t, acc, codes, scales):
+        def product(w, t, acc, codes, scales):
             nc.tensor.matmul_mx(
                 out=acc,
-                lhsT=deal_w[i][:, 2 * P * t : 2 * P * (t + 1)].bitcast(FP4X4),
-                lhsT_scale=deal_s[i][:, P * t : P * (t + 1)],
+                lhsT=dealt_words[w][:, 2 * P * t : 2 * P * (t + 1)].bitcast(FP4X4),
+                lhsT_scale=dealt_scales[w][:, P * t : P * (t + 1)],
                 rhs=codes.bitcast(FP8X4),
                 rhs_scale=scales,
                 start=True,
                 stop=True,
             )
 
-        def interleave(rows, planes, cols):
-            nc.scalar.copy(
-                out=rows[:].rearrange("p (c i) t -> p c t i", i=4),
-                in_=planes[:, :, cols].rearrange("p t (c i) -> p c t i", i=4),
-            )
+        def interleaved(rows, run):
+            return rows.rearrange("p (c i) t -> p c t i", i=run)
+
+        def by_plane(planes, run):
+            return planes.rearrange("p t (c i) -> p c t i", i=run)
+
+        f32_run, bf16_run = 2, 4
 
         def quantize(codes, scales, rows):
             nc.vector.quantize_mx(out=codes.bitcast(FP8X4), scales=scales, in_=rows[:].rearrange("p c t -> p (c t)"))
 
-        halves = [slice(h * HALF, (h + 1) * HALF) for h in range(2)]
-
-        xg_w = []
-        xg_s = held.tile([P, S], U8, name="xg_s", align_bytes=64)
-        deal_words(nc.vector, 0)
-        nc.vector.tensor_copy(out=xg_s[:], in_=xs[:].indirect(offs_sb[:]))
-        deal_scales(nc.vector, 0)
-        for h, cols in enumerate(halves):
-            xg_w.append(held.tile([P, HALF], U32, name="xg_w%d" % h, tag=("xg_w0", "raw_s0")[h], align_bytes=64))
-            nc.vector.tensor_copy(
-                out=xg_w[h][:], in_=xw[:].bitcast(U32).indirect(offs_sb[:, h * HALF // 16 : (h + 1) * HALF // 16])
-            )
-        deal_words(nc.vector, 2)
-        deal_scales(nc.vector, 2)
-        y_acc = [[psum.tile([P, HALF], F32, name="acc") for h in range(2)] for t in range(PACK)]
-        yg = held.tile([P, PACK, S], F32, name="yg")
-        for t in range(PACK):
-            for h, cols in enumerate(halves):
-                product(0, t, y_acc[t][h][:], xg_w[h][:], xg_s[:, cols])
-                nc.scalar.copy(out=y_win[t][:, cols], in_=y_acc[t][h][:])
-        for t in range(PACK):
-            for h, cols in enumerate(halves):
-                nc.scalar.activation(out=yg[:, t, cols], in_=y_acc[t][h][:], func=ACT.Copy, scale=gn_sb[:, t : t + 1])
-
-        def fetched(name, slot):
-            return held.tile([P, S], F32, name=name, tag="fetched%d" % slot, align_bytes=64)
-
-        g3, g4, st_turned = [], [], []
-        z2_planes = held.tile([P, PACK, S], BF16, name="z2_planes", tag="planes")
-        minus_gm = held.tile([P, PACK], F32, name="minus_gm")
-        nc.scalar.activation(out=minus_gm[:], in_=gm_sb[:], func=ACT.Copy, scale=-1.0)
-
-        def turn(bank, src, first, last):
-            for k in range(PACK):
+        def add_turned(acc, plane, opens, closes):
+            for k in range(PLANES):
                 nc.tensor.matmul(
-                    out=bank[:, P * k : P * (k + 1)], lhsT=src[:, P * k : P * (k + 1)], rhs=ident[:], is_transpose=True,
-                    start=first and k == 0, stop=last and k == PACK - 1,
+                    out=acc[:, P * k : P * (k + 1)], lhsT=plane[:, P * k : P * (k + 1)], rhs=ident[:],
+                    is_transpose=True, start=opens and k == 0, stop=closes and k == last,
                 )
 
+        x_picked = []
+        x_picked_scales = held.tile([P, S], U8, name="x_picked_scales", align_bytes=64)
+        deal_words(W1, "dealt_words_w1")
+        nc.vector.tensor_copy(out=x_picked_scales[:], in_=x_table_scales[:].indirect(offs_sb[:]))
+        deal_scales(W1, "dealt_scales_w1")
+        for h in range(2):
+            buffer = ("x_picked0", "raw_scales%d" % W1)[h]
+            x_picked.append(held.tile([P, HALF], U32, name="x_picked%d" % h, tag=buffer, align_bytes=64))
+            nc.vector.tensor_copy(
+                out=x_picked[h][:], in_=x_table[:].bitcast(U32).indirect(entries(offs_sb, h * HALF, HALF))
+            )
+        deal_words(W3, "x_table")
+        y_gained = held.tile([P, PLANES, S], F32, name="y_gained")
+        for t in range(PLANES):
+            for h, cols in enumerate(halves):
+                y_acc = bank((t + 2 * h) % PLANES, HALF)
+                product(W1, t, y_acc[:], x_picked[h][:], x_picked_scales[:, cols])
+                nc.scalar.copy(out=y_win[t][:, cols], in_=y_acc[:])
+        deal_scales(W3, "x_picked_scales")
+        for t in range(PLANES):
+            nc.scalar.activation(out=y_gained[:, t, :], in_=y_win[t][:, :S], func=ACT.Copy, scale=gn_sb[:, t : t + 1])
+
+        shared = held.tile([P, PLANES * S], F32, name="shared", align_bytes=64)
+        sig1 = shared[:].rearrange("p (t c) -> p t c", t=PLANES)
+        z2_planes = shared[:, 2 * S :].bitcast(BF16).rearrange("p (t c) -> p t c", t=PLANES)
+        minus_gm = held.tile([P, PLANES], F32, name="minus_gm")
+        nc.scalar.activation(out=minus_gm[:], in_=gm_sb[:], func=ACT.Copy, scale=-1.0)
+        y_n3, minus_st_n4, minus_st_turned, excess = [], [], [], []
+
         def larger(t):
-            nc.vector.tensor_tensor(out=st_win[t][:, :S], in0=g3[t][:], in1=y_win[t][:, :S], op=ALU.max)
-            bank = psum.tile([P, S], F32, name="acc")
-            turn(bank, st_win[t], True, True)
-            st_turned.append(held.tile([P, S], F32, name="st_turned%d" % t))
-            nc.scalar.activation(out=st_turned[t][:], in_=bank[:], func=ACT.Copy, scale=-1.0)
+            nc.vector.tensor_tensor(out=st_win[t][:, :S], in0=y_n3[t][:], in1=y_win[t][:, :S], op=ALU.max)
+            st_turned = next_bank(S)
+            add_turned(st_turned, st_win[t], True, True)
+            minus_st_turned.append(held.tile([P, S], F32, name="minus_st_turned%d" % t)[:])
+            nc.scalar.activation(out=minus_st_turned[t], in_=st_turned[:], func=ACT.Copy, scale=-1.0)
 
-        def smaller(t):
-            gap = psum.tile([P, S], F32, name="acc")
-            turn(gap, st_win[t], True, False)
-            turn(gap, g4[t], False, True)
-            excess = held.tile([P, S], F32, name="excess%d" % t)
-            nc.scalar.activation(out=excess[:], in_=gap[:], func=ACT.Relu)
-            return excess
+        def find_excess(t):
+            gap = next_bank(S)
+            add_turned(gap, st_win[t], True, False)
+            add_turned(gap, minus_st_n4[t], False, True)
+            if t in (1, 2):
+                excess.append(sig1[:, t - 1, :])
+            else:
+                excess.append(held.tile([P, S], F32, name="excess%d" % t)[:])
+            nc.scalar.activation(out=excess[t], in_=gap[:], func=ACT.Relu)
 
-        def scaled(t, excess):
-            low = psum.tile([P, S], F32, name="acc")
-            turn(low, st_turned[t], True, False)
-            turn(low, excess, False, True)
-            nc.scalar.activation(out=z2_planes[:, t, :], in_=low[:], func=ACT.Copy, scale=minus_gm[:, t : t + 1])
+        def z2_plane(t):
+            minus_low = next_bank(S)
+            add_turned(minus_low, minus_st_turned[t], True, False)
+            add_turned(minus_low, excess[t], False, True)
+            nc.scalar.activation(
+                out=z2_planes[:, t, :], in_=minus_low[:], func=ACT.Copy, scale=minus_gm[:, t : t + 1]
+            )
 
-        for t in range(PACK):
-            g3.append(fetched("g3_%d" % t, t))
-            nc.vector.tensor_copy(out=g3[t][:], in_=y_win[t][:].indirect(n3_sb[:]))
+        for t in range(PLANES):
+            y_n3.append(plane_in("y_n3_%d" % t, "y_n3_%d" % t))
+            nc.vector.tensor_copy(out=y_n3[t][:], in_=y_win[t][:].indirect(n3_sb[:]))
             if t > 0:
                 larger(t - 1)
-        excess = []
-        for t in range(PACK):
-            g4.append(fetched("g4_%d" % t, (6, 7, 8, 12)[t]))
+        for t in range(PLANES):
+            minus_st_n4.append(plane_in("st_n4_%d" % t, "minus_st_n4_%d" % t))
             nc.vector.tensor_scalar(
-                out=g4[t][:], in0=st_win[t][:].indirect(n4_sb[:]), scalar1=-1.0, scalar2=0.0, op0=ALU.mult, op1=ALU.add
+                out=minus_st_n4[t][:], in0=st_win[t][:].indirect(n4_sb[:]),
+                scalar1=-1.0, scalar2=0.0, op0=ALU.mult, op1=ALU.add,
             )
             if t == 0:
-                larger(PACK - 1)
-            excess.append(smaller(t))
+                larger(last)
+            find_excess(t)
             if t > 0:
-                scaled(t - 1, excess[t - 1])
-        scaled(PACK - 1, excess[PACK - 1])
+                z2_plane(t - 1)
+        z2_plane(last)
 
-        z2_bf = [held.tile([P, HALF, PACK], BF16, name="z2_bf%d" % h, tag="fetched%d" % (4 + h), align_bytes=64) for h in range(2)]
-        z2_w = held.tile([P, S], U32, name="z2_w", align_bytes=64)
-        z2_s = held.tile([P, S], U8, name="z2_s", align_bytes=64)
+        z2_rows = [held.tile([P, HALF, PLANES], BF16, name="z2_rows%d" % h, align_bytes=64) for h in range(2)]
+        z2_codes = held.tile([P, S], U32, name="z2_codes", align_bytes=64)
+        z2_scales = held.tile([P, S], U8, name="z2_scales", align_bytes=64)
         for h, cols in enumerate(halves):
-            interleave(z2_bf[h], z2_planes, cols)
+            nc.scalar.copy(out=interleaved(z2_rows[h][:], bf16_run), in_=by_plane(z2_planes[:, :, cols], bf16_run))
 
-        g1 = []
-        diff = []
-        sig1 = held.tile([P, PACK, S], F32, name="sig1", tag="planes")
-        b_acc = [psum.tile([P, S], F32, name="acc") for t in range(PACK)]
-        b_plain = four("b_plain", [P, S], F32)
+        y_n1, diff = [], []
+        b_acc = [next_bank(S) for t in range(PLANES)]
+        b_plain = per_plane("b_plain", S)
 
         def difference(t):
-            diff.append(fetched("diff%d" % t, (9, 10, 11, 5)[t]))
-            nc.vector.tensor_tensor(out=diff[t][:], in0=y_win[t][:].indirect(n2_sb[:]), in1=g1[t][:], op=ALU.subtract)
+            diff.append(plane_in("diff%d" % t, "diff%d" % t))
+            nc.vector.tensor_tensor(out=diff[t][:], in0=y_win[t][:].indirect(n2_sb[:]), in1=y_n1[t][:], op=ALU.subtract)
             nc.scalar.activation(out=sig1[:, t, :], in_=diff[t][:], func=ACT.Sigmoid, scale=-1.0)
 
-        def b_half(h):
-            cols = halves[h]
-            quantize(z2_w[:, cols], z2_s[:, cols], z2_bf[h])
-            for t in range(PACK):
-                product(2, t, b_acc[t][:, cols], z2_w[:, cols], z2_s[:, cols])
-
-        for t in range(PACK):
-            if t == PACK - 1:
-                b_half(0)
-            g1.append(fetched("g1_%d" % t, (3, 2, 1, 4)[t]))
-            nc.vector.tensor_copy(out=g1[t][:], in_=y_win[t][:].indirect(n1_sb[:]))
+        for t in range(PLANES):
+            y_n1.append(plane_in("y_n3_%d" % (last - t), "y_n1_%d" % t))
+            nc.vector.tensor_copy(out=y_n1[t][:], in_=y_win[t][:].indirect(n1_sb[:]))
             if t > 0:
                 difference(t - 1)
-        b_half(1)
-        difference(PACK - 1)
-        deal_words(nc.vector, 1)
-        deal_scales(nc.vector, 1)
-        for t in range(PACK):
+        difference(last)
+
+        for h, cols in enumerate(halves):
+            quantize(z2_codes[:, cols], z2_scales[:, cols], z2_rows[h])
+            for t in range(PLANES):
+                product(W3, t, b_acc[t][:, cols], z2_codes[:, cols], z2_scales[:, cols])
+        deal_words(W2, "z2_rows0")
+        deal_scales(W2, "z2_rows1")
+        for t in range(PLANES):
             nc.scalar.copy(out=st_win[t][:, :S], in_=b_acc[t][:])
             if t == 0:
                 nc.scalar.copy(out=b_plain[t][:], in_=b_acc[t][:])
             else:
                 nc.sync.dma_start(out=b_plain[t][:], in_=st_win[t][:, :S])
 
-        z_bf = [held.tile([P, HALF, PACK], BF16, name="z_bf%d" % h, tag="fetched%d" % (7 + h), align_bytes=64) for h in range(2)]
-        z_w = held.tile([P, S], U32, name="z_w", align_bytes=64)
-        z_s = held.tile([P, S], U8, name="z_s", align_bytes=64)
-        sig2 = held.tile([P, PACK, S], F32, name="sig2")
-        a_acc = [[psum.tile([P, HALF], F32, name="acc") for t in range(PACK)] for h in range(2)]
-        a_win = four("a_win", [P, S], F32)
-        a_plain = four("a_plain", [P, S], F32)
+        z_rows = [
+            held.tile([P, HALF, PLANES], BF16, name="z_rows%d" % h, tag="st_n4_%d" % (1 + h), align_bytes=64)
+            for h in range(2)
+        ]
+        z_codes = held.tile([P, S], U32, name="z_codes", align_bytes=64)
+        z_scales = held.tile([P, S], U8, name="z_scales", align_bytes=64)
+        sig2 = held.tile([P, PLANES, S], F32, name="sig2")
+        a_acc = [[next_bank(HALF) for t in range(PLANES)] for h in range(2)]
+        a_win = per_plane("a_win", S)
+        a_plain = per_plane("a_plain", S)
 
         def gate(t):
-            b_sum = fetched("b_sum%d" % t, (0, 6, 7, 8)[t])
+            b_sum = plane_in("y_n3_0" if t == 0 else "st_n4_%d" % (t - 1), "b_sum%d" % t)
             nc.vector.tensor_tensor(out=b_sum[:], in0=st_win[t][:].indirect(n6_sb[:]), in1=b_plain[t][:], op=ALU.add)
             nc.scalar.activation(out=sig2[:, t, :], in_=b_sum[:], func=ACT.Sigmoid)
 
-        def z_half(h):
+        for h, cols in enumerate(halves):
             nc.vector.tensor_tensor(
-                out=z_bf[h][:].rearrange("p (c i) t -> p c t i", i=2),
-                in0=sig1[:, :, halves[h]].rearrange("p t (c i) -> p c t i", i=2),
-                in1=yg[:, :, halves[h]].rearrange("p t (c i) -> p c t i", i=2),
+                out=interleaved(z_rows[h][:], f32_run),
+                in0=by_plane(sig1[:, :, cols], f32_run),
+                in1=by_plane(y_gained[:, :, cols], f32_run),
                 op=ALU.mult,
             )
-
-        def a_half(h):
-            cols = halves[h]
-            quantize(z_w[:, cols], z_s[:, cols], z_bf[h])
-            for t in range(PACK):
-                product(1, t, a_acc[h][t][:], z_w[:, cols], z_s[:, cols])
-
-        z_half(0)
-        z_half(1)
         gate(0)
-        a_half(0)
-        a_half(1)
+        for h, cols in enumerate(halves):
+            quantize(z_codes[:, cols], z_scales[:, cols], z_rows[h])
+            for t in range(PLANES):
+                product(W2, t, a_acc[h][t][:], z_codes[:, cols], z_scales[:, cols])
         gate(1)
-        for t in range(PACK):
-            nc.scalar.copy(out=a_win[t][:, halves[0]], in_=a_acc[0][t][:])
-            nc.scalar.copy(out=a_win[t][:, halves[1]], in_=a_acc[1][t][:])
+        for t in range(PLANES):
+            for h, cols in enumerate(halves):
+                nc.scalar.copy(out=a_win[t][:, cols], in_=a_acc[h][t][:])
             nc.scalar.copy(out=a_plain[t][:, halves[0]], in_=a_acc[0][t][:])
             nc.sync.dma_start(out=a_plain[t][:, halves[1]], in_=a_win[t][:, halves[1]])
         gate(2)
         gate(3)
 
-        out_w = held.tile([P, S], U32, name="out_w", align_bytes=64)
-        out_s = held.tile([P, S], U8, name="out_s", align_bytes=64)
-        out_rows = out_0.rearrange("(p t) c -> p t c", t=PACK)
+        out_codes = held.tile([P, S], U32, name="out_codes", align_bytes=64)
+        out_scales = held.tile([P, S], U8, name="out_scales", align_bytes=64)
+        out_planes = out_0.rearrange("(p t) c -> p t c", t=PLANES)
         out_words = out_1[0].rearrange("p c r -> p (c r)").bitcast(I32)
-        a_sum = {}
-        rounded = {}
+        out_rows = []
 
-        def fetch(k):
-            c0, width = OUT_CHUNKS[k]
-            a_sum[k] = held.tile([P, PACK, width], F32, name="a_sum%d" % k, tag="a_sum%d" % (k % 2))
-            for t in range(PACK):
+        def finish(r):
+            first, width = OUT_RANGES[r]
+            cols = slice(first, first + width)
+            a_sum = held.tile([P, PLANES, width], F32, name="a_sum%d" % r, tag="a_sum%d" % (r % 2))
+            for t in range(PLANES):
                 nc.vector.tensor_tensor(
-                    out=a_sum[k][:, t, :],
-                    in0=a_win[t][:].indirect(n5_sb[:, c0 // 16 : (c0 + width) // 16]),
-                    in1=a_plain[t][:, c0 : c0 + width],
-                    op=ALU.add,
+                    out=a_sum[:, t, :], in0=a_win[t][:].indirect(entries(n5_sb, first, width)),
+                    in1=a_plain[t][:, cols], op=ALU.add,
                 )
-
-        def combine(k):
-            c0, width = OUT_CHUNKS[k]
-            cols = slice(c0, c0 + width)
-            res = held.tile([P, PACK, width], F32, name="res%d" % k)
-            rounded[k] = held.tile([P, width, PACK], BF16, name="rounded%d" % k, align_bytes=64)
-            nc.vector.tensor_tensor(out=res[:], in0=a_sum[k][:], in1=sig2[:, :, cols], op=ALU.mult)
-            nc.sync.dma_start(out=out_rows[:, :, cols], in_=res[:])
-            dst = rounded[k][:].rearrange("p (c i) t -> p c t i", i=2)
-            src = res[:].rearrange("p t (c i) -> p c t i", i=2)
-            if k == len(OUT_CHUNKS) - 1:
-                nc.vector.tensor_copy(out=dst, in_=src)
+            result = held.tile([P, PLANES, width], F32, name="result%d" % r)
+            out_rows.append(held.tile([P, width, PLANES], BF16, name="out_rows%d" % r, align_bytes=64))
+            nc.vector.tensor_tensor(out=result[:], in0=a_sum[:], in1=sig2[:, :, cols], op=ALU.mult)
+            nc.sync.dma_start(out=out_planes[:, :, cols], in_=result[:])
+            if r == len(OUT_RANGES) - 1:
+                nc.vector.tensor_copy(out=interleaved(out_rows[r][:], f32_run), in_=by_plane(result[:], f32_run))
             else:
-                nc.scalar.copy(out=dst, in_=src)
+                nc.scalar.copy(out=interleaved(out_rows[r][:], f32_run), in_=by_plane(result[:], f32_run))
 
-        def hand_on(k):
-            c0, width = OUT_CHUNKS[k]
-            cols = slice(c0, c0 + width)
-            quantize(out_w[:, cols], out_s[:, cols], rounded[k])
-            nc.sync.dma_start(out=out_words[:, cols], in_=out_w[:, cols].bitcast(I32))
+        def hand_on(r):
+            first, width = OUT_RANGES[r]
+            cols = slice(first, first + width)
+            quantize(out_codes[:, cols], out_scales[:, cols], out_rows[r])
+            nc.sync.dma_start(out=out_words[:, cols], in_=out_codes[:, cols].bitcast(I32))
 
-        fetch(0)
-        combine(0)
-        fetch(1)
-        combine(1)
-        hand_on(0)
-        fetch(2)
-        combine(2)
-        hand_on(1)
-        hand_on(2)
-        for q in range(4):
+        for r in range(len(OUT_RANGES)):
+            finish(r)
+            if r > 0:
+                hand_on(r - 1)
+        hand_on(len(OUT_RANGES) - 1)
+        for q in range(QUADRANTS):
             queue = nc.scalar if q % 2 else nc.sync
-            queue.dma_start(out=out_2[0, 4 * q : 4 * q + 4, :].bitcast(I32), in_=out_s[32 * q : 32 * q + 4, :].bitcast(I32))
+            queue.dma_start(
+                out=out_2[0, 4 * q : 4 * q + 4, :].bitcast(I32), in_=out_scales[32 * q : 32 * q + 4, :].bitcast(I32)
+            )

from contextlib import ExitStack

import concourse.mybir as mybir
from concourse.masks import make_identity

T = 2048
S = 512
H = 512
FLOPS = 3 * 2 * 512 * 512 * 512

F32 = mybir.dt.float32
BF16 = mybir.dt.bfloat16
I32 = mybir.dt.int32
U32 = mybir.dt.uint32
U16 = mybir.dt.uint16
U8 = mybir.dt.uint8
FP8X4 = mybir.dt.float8_e4m3fn_x4
FP4X4 = mybir.dt.float4_e2m1fn_x4
ALU = mybir.AluOpType
ACT = mybir.ActivationFunctionType

P = 128
PLANES = 4
QUADRANTS = 4
BANKS = 8
HALF = S // 2
STRIPE = 16
W1, W2, W3 = 0, 1, 2
OUT_RANGES = ((0, 256), (256, 128), (384, 128))


def load_scale_rows(nc, scale_tile, rows):
    for q in range(QUADRANTS):
        nc.sync.dma_start(
            out=scale_tile[32 * q : 32 * q + 4, :].bitcast(I32), in_=rows[0, 4 * q : 4 * q + 4, :].bitcast(I32)
        )


def tile_picked_forktriebcmphopmn_none_po_kernel(
    tc, x_words, x_scales, w1_words, w1_scales, gn, w2_words, w2_scales, gm, w3_words, w3_scales,
    offs, n1, n2, n3, n4, n5, n6, out_0, out_1, out_2,
):
    nc = tc.nc
    with ExitStack() as ctx:
        held = ctx.enter_context(tc.tile_pool(name="held", bufs=1))
        psum = ctx.enter_context(tc.psum_pool(name="psum", bufs=1))
        halves = [slice(h * HALF, (h + 1) * HALF) for h in range(2)]
        last = PLANES - 1

        def bank(number, width):
            return psum.tile([P, width], F32, name="bank%d" % number)

        banks_taken = []

        def next_bank(width):
            banks_taken.append(width)
            return bank((PLANES + len(banks_taken) - 1) % BANKS, width)

        def per_plane(name, width):
            return [held.tile([P, width], F32, name="%s%d" % (name, t), align_bytes=64) for t in range(PLANES)]

        def plane_in(buffer, name):
            return held.tile([P, S], F32, name=name, tag=buffer, align_bytes=64)

        def entries(list_tile, first, count):
            return list_tile[:, first // STRIPE : (first + count) // STRIPE]

        offs_sb = held.tile([P, S // STRIPE], U16, name="offs_sb")
        n1_sb, n2_sb, n3_sb, n4_sb, n5_sb, n6_sb = [
            held.tile([P, S // STRIPE], U16, name="n%d_sb" % i) for i in range(1, 7)
        ]
        x_table = held.tile([P, T], I32, name="x_table", align_bytes=64)
        x_table_scales = held.tile([P, T], U8, name="x_table_scales", align_bytes=64)
        raw_words = [held.tile([P, 2 * H], U8, name="raw_words%d" % w, align_bytes=64) for w in (W1, W2, W3)]
        raw_scales = [held.tile([P, H], U8, name="raw_scales%d" % w, align_bytes=64) for w in (W1, W2, W3)]
        gn_sb = held.tile([P, PLANES], F32, name="gn_sb")
        gm_sb = held.tile([P, PLANES], F32, name="gm_sb")
        y_win = per_plane("y_win", 2 * S)
        st_win = per_plane("st_win", 2 * S)

        nc.vector.memset(x_table_scales[:, : T // 2].bitcast(I32), 0)
        nc.gpsimd.memset(x_table_scales[:, T // 2 :].bitcast(I32), 0)
        for w in (W1, W2, W3):
            nc.vector.memset(raw_scales[w][:].bitcast(I32), 0)

        ident = held.tile([P, P], F32, name="ident")
        make_identity(nc, ident[:])

        w_words = (w1_words, w2_words, w3_words)
        w_scales = (w1_scales, w2_scales, w3_scales)

        def load_words(w):
            nc.sync.dma_start(out=raw_words[w][:].bitcast(I32), in_=w_words[w][0].bitcast(I32))

        nc.sync.dma_start(offs_sb[:], offs)
        load_words(W1)
        nc.sync.dma_start(n3_sb[:], n3)
        load_scale_rows(nc, x_table_scales, x_scales)
        nc.sync.dma_start(out=x_table[:], in_=x_words[0].rearrange("p c r -> p (c r)").bitcast(I32))
        load_scale_rows(nc, raw_scales[W1], w_scales[W1])
        load_words(W3)
        nc.sync.dma_start(n4_sb[:], n4)
        nc.sync.dma_start(out=gm_sb[:], in_=gm.rearrange("(p t) o -> p (t o)", t=PLANES))
        nc.sync.dma_start(out=gn_sb[:], in_=gn.rearrange("(p t) o -> p (t o)", t=PLANES))
        load_scale_rows(nc, raw_scales[W3], w_scales[W3])
        nc.sync.dma_start(n1_sb[:], n1)
        nc.sync.dma_start(n2_sb[:], n2)
        load_words(W2)
        load_scale_rows(nc, raw_scales[W2], w_scales[W2])
        nc.sync.dma_start(n6_sb[:], n6)
        nc.sync.dma_start(n5_sb[:], n5)

        dealt_words = {}
        dealt_scales = {}

        def deal_words(w, buffer):
            dealt_words[w] = held.tile([P, 2 * H], U8, name="dealt_words%d" % w, tag=buffer, align_bytes=64)
            nc.vector.tensor_copy(
                out=dealt_words[w][:].rearrange("p (t m b) -> p t m b", t=PLANES, b=2),
                in_=raw_words[w][:].rearrange("p (m t b) -> p t m b", t=PLANES, b=2),
            )

        def deal_scales(w, buffer):
            dealt_scales[w] = held.tile([P, H], U8, name="dealt_scales%d" % w, tag=buffer, align_bytes=64)
            nc.vector.tensor_copy(
                out=dealt_scales[w][:].rearrange("p (t m) -> p t m", t=PLANES),
                in_=raw_scales[w][:].rearrange("p (m t) -> p t m", t=PLANES),
            )

        def product(w, t, acc, codes, scales):
            nc.tensor.matmul_mx(
                out=acc,
                lhsT=dealt_words[w][:, 2 * P * t : 2 * P * (t + 1)].bitcast(FP4X4),
                lhsT_scale=dealt_scales[w][:, P * t : P * (t + 1)],
                rhs=codes.bitcast(FP8X4),
                rhs_scale=scales,
                start=True,
                stop=True,
            )

        def interleaved(rows, run):
            return rows.rearrange("p (c i) t -> p c t i", i=run)

        def by_plane(planes, run):
            return planes.rearrange("p t (c i) -> p c t i", i=run)

        f32_run, bf16_run = 2, 4

        def quantize(codes, scales, rows):
            nc.vector.quantize_mx(out=codes.bitcast(FP8X4), scales=scales, in_=rows[:].rearrange("p c t -> p (c t)"))

        def add_turned(acc, plane, opens, closes):
            for k in range(PLANES):
                nc.tensor.matmul(
                    out=acc[:, P * k : P * (k + 1)], lhsT=plane[:, P * k : P * (k + 1)], rhs=ident[:],
                    is_transpose=True, start=opens and k == 0, stop=closes and k == last,
                )

        x_picked = []
        x_picked_scales = held.tile([P, S], U8, name="x_picked_scales", align_bytes=64)
        deal_words(W1, "dealt_words_w1")
        nc.vector.tensor_copy(out=x_picked_scales[:], in_=x_table_scales[:].indirect(offs_sb[:]))
        deal_scales(W1, "dealt_scales_w1")
        for h in range(2):
            buffer = ("x_picked0", "raw_scales%d" % W1)[h]
            x_picked.append(held.tile([P, HALF], U32, name="x_picked%d" % h, tag=buffer, align_bytes=64))
            nc.vector.tensor_copy(
                out=x_picked[h][:], in_=x_table[:].bitcast(U32).indirect(entries(offs_sb, h * HALF, HALF))
            )
        deal_words(W3, "x_table")
        y_gained = held.tile([P, PLANES, S], F32, name="y_gained")
        for t in range(PLANES):
            for h, cols in enumerate(halves):
                y_acc = bank((t + 2 * h) % PLANES, HALF)
                product(W1, t, y_acc[:], x_picked[h][:], x_picked_scales[:, cols])
                nc.scalar.copy(out=y_win[t][:, cols], in_=y_acc[:])
        deal_scales(W3, "x_picked_scales")
        for t in range(PLANES):
            nc.scalar.activation(out=y_gained[:, t, :], in_=y_win[t][:, :S], func=ACT.Copy, scale=gn_sb[:, t : t + 1])

        shared = held.tile([P, PLANES * S], F32, name="shared", align_bytes=64)
        sig1 = shared[:].rearrange("p (t c) -> p t c", t=PLANES)
        z2_planes = shared[:, 2 * S :].bitcast(BF16).rearrange("p (t c) -> p t c", t=PLANES)
        minus_gm = held.tile([P, PLANES], F32, name="minus_gm")
        nc.scalar.activation(out=minus_gm[:], in_=gm_sb[:], func=ACT.Copy, scale=-1.0)
        y_n3, minus_st_n4, minus_st_turned, excess = [], [], [], []

        def larger(t):
            nc.vector.tensor_tensor(out=st_win[t][:, :S], in0=y_n3[t][:], in1=y_win[t][:, :S], op=ALU.max)
            st_turned = next_bank(S)
            add_turned(st_turned, st_win[t], True, True)
            minus_st_turned.append(held.tile([P, S], F32, name="minus_st_turned%d" % t)[:])
            nc.scalar.activation(out=minus_st_turned[t], in_=st_turned[:], func=ACT.Copy, scale=-1.0)

        def find_excess(t):
            gap = next_bank(S)
            add_turned(gap, st_win[t], True, False)
            add_turned(gap, minus_st_n4[t], False, True)
            if t in (1, 2):
                excess.append(sig1[:, t - 1, :])
            else:
                excess.append(held.tile([P, S], F32, name="excess%d" % t)[:])
            nc.scalar.activation(out=excess[t], in_=gap[:], func=ACT.Relu)

        def z2_plane(t):
            minus_low = next_bank(S)
            add_turned(minus_low, minus_st_turned[t], True, False)
            add_turned(minus_low, excess[t], False, True)
            nc.scalar.activation(
                out=z2_planes[:, t, :], in_=minus_low[:], func=ACT.Copy, scale=minus_gm[:, t : t + 1]
            )

        for t in range(PLANES):
            y_n3.append(plane_in("y_n3_%d" % t, "y_n3_%d" % t))
            nc.vector.tensor_copy(out=y_n3[t][:], in_=y_win[t][:].indirect(n3_sb[:]))
            if t > 0:
                larger(t - 1)
        for t in range(PLANES):
            minus_st_n4.append(plane_in("st_n4_%d" % t, "minus_st_n4_%d" % t))
            nc.vector.tensor_scalar(
                out=minus_st_n4[t][:], in0=st_win[t][:].indirect(n4_sb[:]),
                scalar1=-1.0, scalar2=0.0, op0=ALU.mult, op1=ALU.add,
            )
            if t == 0:
                larger(last)
            find_excess(t)
            if t > 0:
                z2_plane(t - 1)
        z2_plane(last)

        z2_rows = [held.tile([P, HALF, PLANES], BF16, name="z2_rows%d" % h, align_bytes=64) for h in range(2)]
        z2_codes = held.tile([P, S], U32, name="z2_codes", align_bytes=64)
        z2_scales = held.tile([P, S], U8, name="z2_scales", align_bytes=64)
        for h, cols in enumerate(halves):
            nc.scalar.copy(out=interleaved(z2_rows[h][:], bf16_run), in_=by_plane(z2_planes[:, :, cols], bf16_run))

        y_n1, diff = [], []
        b_acc = [next_bank(S) for t in range(PLANES)]
        b_plain = per_plane("b_plain", S)

        def difference(t):
            diff.append(plane_in("diff%d" % t, "diff%d" % t))
            nc.vector.tensor_tensor(out=diff[t][:], in0=y_win[t][:].indirect(n2_sb[:]), in1=y_n1[t][:], op=ALU.subtract)
            nc.scalar.activation(out=sig1[:, t, :], in_=diff[t][:], func=ACT.Sigmoid, scale=-1.0)

        for t in range(PLANES):
            y_n1.append(plane_in("y_n3_%d" % (last - t), "y_n1_%d" % t))
            nc.vector.tensor_copy(out=y_n1[t][:], in_=y_win[t][:].indirect(n1_sb[:]))
            if t > 0:
                difference(t - 1)
        difference(last)

        for h, cols in enumerate(halves):
            quantize(z2_codes[:, cols], z2_scales[:, cols], z2_rows[h])
            for t in range(PLANES):
                product(W3, t, b_acc[t][:, cols], z2_codes[:, cols], z2_scales[:, cols])
        deal_words(W2, "z2_rows0")
        deal_scales(W2, "z2_rows1")
        for t in range(PLANES):
            nc.scalar.copy(out=st_win[t][:, :S], in_=b_acc[t][:])
            if t == 0:
                nc.scalar.copy(out=b_plain[t][:], in_=b_acc[t][:])
            else:
                nc.sync.dma_start(out=b_plain[t][:], in_=st_win[t][:, :S])

        z_rows = [
            held.tile([P, HALF, PLANES], BF16, name="z_rows%d" % h, tag="st_n4_%d" % (1 + h), align_bytes=64)
            for h in range(2)
        ]
        z_codes = held.tile([P, S], U32, name="z_codes", align_bytes=64)
        z_scales = held.tile([P, S], U8, name="z_scales", align_bytes=64)
        sig2 = held.tile([P, PLANES, S], F32, name="sig2")
        a_acc = [[next_bank(HALF) for t in range(PLANES)] for h in range(2)]
        a_win = per_plane("a_win", S)
        a_plain = per_plane("a_plain", S)

        def gate(t):
            b_sum = plane_in("y_n3_0" if t == 0 else "st_n4_%d" % (t - 1), "b_sum%d" % t)
            nc.vector.tensor_tensor(out=b_sum[:], in0=st_win[t][:].indirect(n6_sb[:]), in1=b_plain[t][:], op=ALU.add)
            nc.scalar.activation(out=sig2[:, t, :], in_=b_sum[:], func=ACT.Sigmoid)

        for h, cols in enumerate(halves):
            nc.vector.tensor_tensor(
                out=interleaved(z_rows[h][:], f32_run),
                in0=by_plane(sig1[:, :, cols], f32_run),
                in1=by_plane(y_gained[:, :, cols], f32_run),
                op=ALU.mult,
            )
        gate(0)
        for h, cols in enumerate(halves):
            quantize(z_codes[:, cols], z_scales[:, cols], z_rows[h])
            for t in range(PLANES):
                product(W2, t, a_acc[h][t][:], z_codes[:, cols], z_scales[:, cols])
        gate(1)
        for t in range(PLANES):
            for h, cols in enumerate(halves):
                nc.scalar.copy(out=a_win[t][:, cols], in_=a_acc[h][t][:])
            nc.scalar.copy(out=a_plain[t][:, halves[0]], in_=a_acc[0][t][:])
            nc.sync.dma_start(out=a_plain[t][:, halves[1]], in_=a_win[t][:, halves[1]])
        gate(2)
        gate(3)

        out_codes = held.tile([P, S], U32, name="out_codes", align_bytes=64)
        out_scales = held.tile([P, S], U8, name="out_scales", align_bytes=64)
        out_planes = out_0.rearrange("(p t) c -> p t c", t=PLANES)
        out_words = out_1[0].rearrange("p c r -> p (c r)").bitcast(I32)
        out_rows = []

        def finish(r):
            first, width = OUT_RANGES[r]
            cols = slice(first, first + width)
            a_sum = held.tile([P, PLANES, width], F32, name="a_sum%d" % r, tag="a_sum%d" % (r % 2))
            for t in range(PLANES):
                nc.vector.tensor_tensor(
                    out=a_sum[:, t, :], in0=a_win[t][:].indirect(entries(n5_sb, first, width)),
                    in1=a_plain[t][:, cols], op=ALU.add,
                )
            result = held.tile([P, PLANES, width], F32, name="result%d" % r)
            out_rows.append(held.tile([P, width, PLANES], BF16, name="out_rows%d" % r, align_bytes=64))
            nc.vector.tensor_tensor(out=result[:], in0=a_sum[:], in1=sig2[:, :, cols], op=ALU.mult)
            nc.sync.dma_start(out=out_planes[:, :, cols], in_=result[:])
            if r == len(OUT_RANGES) - 1:
                nc.vector.tensor_copy(out=interleaved(out_rows[r][:], f32_run), in_=by_plane(result[:], f32_run))
            else:
                nc.scalar.copy(out=interleaved(out_rows[r][:], f32_run), in_=by_plane(result[:], f32_run))

        def hand_on(r):
            first, width = OUT_RANGES[r]
            cols = slice(first, first + width)
            quantize(out_codes[:, cols], out_scales[:, cols], out_rows[r])
            nc.sync.dma_start(out=out_words[:, cols], in_=out_codes[:, cols].bitcast(I32))

        for r in range(len(OUT_RANGES)):
            finish(r)
            if r > 0:
                hand_on(r - 1)
        hand_on(len(OUT_RANGES) - 1)
        for q in range(QUADRANTS):
            queue = nc.scalar if q % 2 else nc.sync
            queue.dma_start(
                out=out_2[0, 4 * q : 4 * q + 4, :].bitcast(I32), in_=out_scales[32 * q : 32 * q + 4, :].bitcast(I32)
            )
